import numpy as np
import ml_dtypes


def mxq(x, axis, fmt="e4m3"):
    dtype, down = {"e4m3": (ml_dtypes.float8_e4m3fn, 7), "e5m2": (ml_dtypes.float8_e5m2, 14)}[fmt]
    v = np.moveaxis(np.asarray(x, np.float32).astype(ml_dtypes.bfloat16).astype(np.float64), axis, -1)
    blocks = v.reshape(v.shape[:-1] + (-1, 32))
    amax = np.abs(blocks).max(-1, keepdims=True)
    byte = np.maximum(np.where(amax > 0, np.frexp(amax)[1] - 1 + 127, 0) - down, 1)
    scale = np.exp2(byte - 127.0)
    codes = (blocks / scale).astype(np.float32).astype(dtype).astype(np.float64)
    return np.moveaxis((codes * scale).reshape(v.shape), -1, axis)


WIDE = False


def mx_kscale(k):
    if not WIDE:
        return np.ones(k)
    levels = np.array([24, -24, 12, -12, 0])
    if k % 512:
        return np.exp2(np.random.permutation(np.resize(levels, k // 32))).repeat(32)
    a = np.empty((k // 512, 16))
    for p in range(k // 512):
        a[p, :8] = np.random.permutation(np.resize(levels, 8))
        for g in range(8):
            far = levels[np.abs(levels - a[p, g]) >= 10]
            a[p, g + 8] = far[np.random.randint(len(far))]
    return np.exp2(a.ravel()).repeat(32)


def f64(x):
    return np.asarray(x).astype(np.float64)


def striped(idx):
    return np.tile(idx.reshape(-1, 16).T, (8, 1)).astype(np.uint16)


def unstriped(offs):
    return offs[:16].T.reshape(-1).astype(np.int64)


E2M1 = np.array([0.0, 0.5, 1.0, 1.5, 2.0, 3.0, 4.0, 6.0, -0.0, -0.5, -1.0, -1.5, -2.0, -3.0, -4.0, -6.0])


def pack_weight(w, fmt):
    k, n = w.shape
    w = f64(np.asarray(w, np.float32).astype(ml_dtypes.bfloat16)).reshape(k // 32, 32, n)
    amax = np.abs(w).max(1)
    if fmt == "e4m3":
        byte = np.frexp(amax)[1] - 1 + 127 - 7
    else:
        mant, ex = np.frexp(amax / 6.0)
        byte = np.where(mant > 0.5, ex, ex - 1) + 127
    byte = np.clip(np.where(amax > 0, byte, 1), 1, 254)
    scaled = (w * np.exp2(127.0 - byte)[:, None, :]).reshape(k, n).astype(np.float32)
    by_word = np.ascontiguousarray(scaled.reshape(k // 512, 128, 4, n).transpose(0, 1, 3, 2))
    if fmt == "e4m3":
        words = by_word.astype(ml_dtypes.float8_e4m3fn).view(np.uint8)
    else:
        c = by_word.astype(ml_dtypes.float4_e2m1fn).view(np.uint8) & 0xF
        words = (c[..., 0::2] | (c[..., 1::2] << 4)).reshape(k // 512, 128, 2 * n)
    return np.ascontiguousarray(words), np.ascontiguousarray(byte.astype(np.uint8).reshape(k // 512, 16, n))


def unpack_weight(words, scales, fmt):
    g, _, n = scales.shape
    words = np.ascontiguousarray(words).reshape(g, 128, n, -1)
    if fmt == "e4m3":
        vals = words.view(ml_dtypes.float8_e4m3fn).astype(np.float64)
    else:
        nib = np.empty((g, 128, n, 4), np.uint8)
        nib[..., 0::2] = words & 0xF
        nib[..., 1::2] = words >> 4
        vals = E2M1[nib]
    vals = vals * np.repeat(np.exp2(scales.astype(np.float64) - 127.0), 8, axis=1)[..., None]
    return vals.transpose(0, 1, 3, 2).reshape(g * 512, n)


def pack_table4(v):
    words, scales = pack_weight(v, "e2m1")
    g, t = words.shape[0] // 2, v.shape[1]
    return np.ascontiguousarray(words.reshape(g, 2, 128, t, 2).transpose(0, 2, 3, 1, 4).reshape(g, 128, t, 4)), scales


def unpack_table4(words, scales):
    g, _, t, _ = words.shape
    return unpack_weight(words.reshape(g, 128, t, 2, 2).transpose(0, 3, 1, 2, 4).reshape(2 * g, 128, 2 * t), scales, "e2m1")


K, L, R, N, T, J = 1024, 512, 512, 256, 4096, 2048


def setup_inputs():
    n = np.random.standard_normal
    s = mx_kscale(K)[:, None]
    s2 = mx_kscale(L)[:, None]
    u = mx_kscale(R)[:, None]
    p_tab = pack_table4(n((K, T)) * s)
    p_tab2 = pack_weight(n((L, T)) * s2, "e4m3")
    p_wa = pack_weight(n((K, R)) / np.sqrt(K) / s * u.T, "e2m1")
    p_wb = pack_weight(n((L, R)) / np.sqrt(L) / s2 * u.T, "e2m1")
    p_en = pack_weight(n((R, N)) / np.sqrt(R) / u, "e2m1")
    return {
        "tab_words": p_tab[0],
        "tab_scales": p_tab[1],
        "tab2_words": p_tab2[0],
        "tab2_scales": p_tab2[1],
        "wa_words": p_wa[0],
        "wa_scales": p_wa[1],
        "wb_words": p_wb[0],
        "wb_scales": p_wb[1],
        "en_words": p_en[0],
        "en_scales": p_en[1],
        "offs": striped(np.random.permutation(T)[:J]),
        "offs2": striped(np.random.permutation(T)[:J]),
    }


def reference(tab_words, tab_scales, tab2_words, tab2_scales, wa_words, wa_scales, wb_words, wb_scales, en_words, en_scales, offs, offs2):
    idx = unstriped(offs)
    idx2 = unstriped(offs2)
    tab_ = unpack_table4(tab_words, tab_scales)[:, idx]
    tab2_ = unpack_weight(tab2_words, tab2_scales, "e4m3")[:, idx2]
    wa_ = unpack_weight(wa_words, wa_scales, "e2m1")
    wb_ = unpack_weight(wb_words, wb_scales, "e2m1")
    ha = wa_.T @ tab_
    hb = wb_.T @ tab2_
    h = np.abs(ha - hb)
    h_ = mxq(h, 0, "e4m3")
    en_ = unpack_weight(en_words, en_scales, "e2m1")
    y = en_.T @ h_
    return y

@@ -1,0 +1,198 @@
+from contextlib import ExitStack
+
+import concourse.mybir as mybir
+
+K, L, R, N, T, J = 1024, 512, 512, 256, 4096, 2048
+FLOPS = 2 * J * R * (K + L + N)
+
+F32 = mybir.dt.float32
+BF16 = mybir.dt.bfloat16
+I32 = mybir.dt.int32
+U32 = mybir.dt.uint32
+U16 = mybir.dt.uint16
+U8 = mybir.dt.uint8
+FP8X4 = mybir.dt.float8_e4m3fn_x4
+FP4X4 = mybir.dt.float4_e2m1fn_x4
+ABS = mybir.ActivationFunctionType.Abs
+SUB = mybir.AluOpType.subtract
+
+P = 128
+PACK = 4
+CHUNK = 512
+CHUNKS = J // CHUNK
+TILE = 128
+TILES = CHUNK // TILE
+COLS = CHUNK // 16
+
+
+def tile_list_kg_absd_none_kernel(
+    tc, tab_words, tab_scales, tab2_words, tab2_scales, wa_words, wa_scales, wb_words, wb_scales,
+    en_words, en_scales, offs, offs2, out,
+):
+    nc = tc.nc
+    with ExitStack() as ctx:
+        lists = ctx.enter_context(tc.tile_pool(name="lists", bufs=1))
+        keep = ctx.enter_context(tc.tile_pool(name="keep", bufs=1))
+        ring = ctx.enter_context(tc.tile_pool(name="ring", bufs=2))
+        psum = ctx.enter_context(tc.psum_pool(name="psum", bufs=2))
+
+        def held(shape, dtype, tag):
+            return keep.tile(shape, dtype, name=tag, tag=tag, align_bytes=64)
+
+        def zero(tile):
+            nc.vector.memset(tile[:].bitcast(I32), 0)
+
+        list_a = lists.tile([P, J // 16], U16, name="list_a")
+        list_b = lists.tile([P, J // 16], U16, name="list_b")
+
+        tab2_plane = held([P, T], U8, "tab2_plane")
+        wb_plane_raw = held([P, R], U8, "wb_plane_raw")
+        tab_plane = held([P, T], U8, "tab_plane")
+        wa_plane_raw = held([P, 2 * R], U8, "wa_plane_raw")
+        en_plane = held([P, N], U8, "en_plane")
+        va_planes = [held([P, J], U8, "va_plane%d" % a) for a in range(2)]
+        zero(tab2_plane)
+        nc.vector.memset(tab_plane[32:64, :].bitcast(I32), 0)
+        nc.vector.memset(tab_plane[64:128, :].bitcast(I32), 0)
+        for tile in (wb_plane_raw, wa_plane_raw, en_plane, va_planes[0], va_planes[1]):
+            zero(tile)
+
+        wb_raw = held([P, 2 * R], U8, "wb_raw")
+        tab2_win = held([P, T], U32, "tab2_win")
+        nc.sync.dma_start(list_a[:], offs)
+        nc.sync.dma_start(tab_plane[0:32, :].bitcast(I32), tab_scales.rearrange("a q t -> (a q) t").bitcast(I32))
+        nc.sync.dma_start(list_b[:], offs2)
+        nc.sync.dma_start(wb_raw[:].bitcast(I32), wb_words[0].bitcast(I32))
+        nc.sync.dma_start(tab2_win[:].bitcast(I32), tab2_words[0].rearrange("p t b -> p (t b)").bitcast(I32))
+        for q in range(4):
+            nc.scalar.dma_start(tab2_plane[32 * q : 32 * q + 4, :].bitcast(I32), tab2_scales[0, 4 * q : 4 * q + 4, :].bitcast(I32))
+        for q in range(4):
+            nc.scalar.dma_start(wb_plane_raw[32 * q : 32 * q + 4, :].bitcast(I32), wb_scales[0, 4 * q : 4 * q + 4, :].bitcast(I32))
+        for q in range(4):
+            nc.sync.dma_start(
+                wa_plane_raw[32 * q : 32 * q + 4, :].bitcast(I32).rearrange("p (a c) -> p a c", a=2),
+                wa_scales[:, 4 * q : 4 * q + 4, :].bitcast(I32).rearrange("a p c -> p a c"),
+            )
+        for q in range(4):
+            nc.sync.dma_start(en_plane[32 * q : 32 * q + 4, :].bitcast(I32), en_scales[0, 4 * q : 4 * q + 4, :].bitcast(I32))
+
+        def gather(window, offsets, c0, c1, dtype, tag):
+            got = held([P, (c1 - c0) * CHUNK], dtype, tag)
+            nc.vector.tensor_copy(got[:], window[:].indirect(offsets[:, c0 * COLS : c1 * COLS]))
+            return got
+
+        def by_slices(raw, passes, dtype, tag):
+            done = held(list(raw.shape), U8, tag)
+            nc.vector.tensor_copy(
+                done[:].bitcast(dtype).rearrange("p (a t m) -> p a t m", a=passes, t=PACK),
+                raw[:].bitcast(dtype).rearrange("p (a m t) -> p a t m", a=passes, t=PACK),
+            )
+            return done
+
+        va_rows = gather(tab_plane, list_a, 0, CHUNKS, U8, "va_rows")
+        for a in range(2):
+            for q in range(4):
+                row = 16 * a + 4 * q
+                nc.sync.dma_start(va_planes[a][32 * q : 32 * q + 4, :].bitcast(I32), va_rows[row : row + 4, :].bitcast(I32))
+        vb_planes = [gather(tab2_plane, list_b, c, c + 1, U8, "vb_plane%d" % c) for c in range(2)]
+        wb = by_slices(wb_raw, 1, U16, "wb")
+        wb_plane = by_slices(wb_plane_raw, 1, U8, "wb_plane")
+
+        tab_win = held([P, T], U32, "wb_raw")
+        nc.sync.dma_start(tab_win[:].bitcast(I32), tab_words[0].rearrange("p t b -> p (t b)").bitcast(I32))
+        wa_raw = held([P, 4 * R], U8, "wb_plane_raw")
+        nc.sync.dma_start(wa_raw[:].bitcast(I32).rearrange("p (a c) -> p a c", a=2), wa_words.bitcast(I32).rearrange("a p c -> p a c"))
+
+        hb_tiles = []
+
+        def relation(c):
+            vb = gather(tab2_win, list_b, c, c + 1, U32, "vb%d" % (c % 2))
+            for i in range(TILES):
+                cols = slice(i * TILE, (i + 1) * TILE)
+                bank = psum.tile([P, PACK, TILE], F32, name="hb_bank", tag="hb_bank", bufs=3)
+                for t in range(PACK):
+                    nc.tensor.matmul_mx(
+                        bank[:, t, :],
+                        lhsT=wb[:, 2 * P * t : 2 * P * (t + 1)].bitcast(FP4X4),
+                        lhsT_scale=wb_plane[:, P * t : P * (t + 1)],
+                        rhs=vb[:, cols].bitcast(FP8X4),
+                        rhs_scale=vb_planes[c][:, cols],
+                        start=True,
+                        stop=True,
+                    )
+                hb = ring.tile([P, TILE, PACK], F32, name="hb", tag="hb", bufs=CHUNKS * TILES)
+                nc.scalar.copy(hb[:], bank[:].rearrange("p t j -> p j t"))
+                hb_tiles.append(hb)
+
+        relation(0)
+        relation(1)
+        for c in (2, 3):
+            vb_planes.append(gather(tab2_plane, list_b, c, c + 1, U8, "vb_plane%d" % (c % 2)))
+            relation(c)
+        wa = by_slices(wa_raw, 2, U16, "wa")
+        wa_plane = by_slices(wa_plane_raw, 2, U8, "wa_plane")
+        en = held([P, 2 * N], U8, "wb_plane_raw")
+        nc.sync.dma_start(en[:].bitcast(I32), en_words[0].bitcast(I32))
+        out_v = out.rearrange("(h n) j -> n h j", h=2)
+
+        def heads(c):
+            pair = gather(tab_win, list_a, c, c + 1, U32, "va_pair")
+            va = ring.tile([P, 4 * CHUNK], U8, name="va", tag="va", align_bytes=64)
+            nc.vector.tensor_copy(
+                va[:].bitcast(U16).rearrange("p (d j) -> p d j", d=2),
+                pair[:].bitcast(U16).rearrange("p (j d) -> p d j", d=2),
+            )
+            return va
+
+        def join(c, i, va, h):
+            j0 = c * CHUNK + i * TILE
+            bank = psum.tile([P, PACK, TILE], F32, name="ha_bank", tag="ha_bank", bufs=3)
+            for t in range(PACK):
+                for a in range(2):
+                    nc.tensor.matmul_mx(
+                        bank[:, t, :],
+                        lhsT=wa[:, 2 * (R * a + P * t) : 2 * (R * a + P * (t + 1))].bitcast(FP4X4),
+                        lhsT_scale=wa_plane[:, R * a + P * t : R * a + P * (t + 1)],
+                        rhs=va[:, 2 * (CHUNK * a + TILE * i) : 2 * (CHUNK * a + TILE * (i + 1))].bitcast(FP4X4),
+                        rhs_scale=va_planes[a][:, j0 : j0 + TILE],
+                        start=(a == 0),
+                        stop=(a == 1),
+                    )
+            diff = ring.tile([P, TILE, PACK], F32, name="diff", tag="diff", bufs=4)
+            nc.vector.tensor_tensor(diff[:], bank[:].rearrange("p t j -> p j t"), hb_tiles[c * TILES + i][:], SUB)
+            nc.scalar.activation(h, diff[:].rearrange("p j t -> p (j t)"), ABS)
+
+        def score(h, j0, width):
+            codes = ring.tile([P, width], U32, name="codes", tag="codes", align_bytes=64, bufs=3)
+            plane = ring.tile([P, width], U8, name="plane", tag="plane", align_bytes=64, bufs=3)
+            nc.vector.quantize_mx(codes[:].bitcast(FP8X4), plane[:], h)
+            y = ring.tile([P, 2, width], F32, name="y", tag="y", bufs=3)
+            per_bank = min(2, 512 // width)
+            for h0 in range(0, 2, per_bank):
+                bank = psum.tile([P, per_bank, width], F32, name="y_bank", tag="y_bank")
+                for g in range(per_bank):
+                    n0 = (h0 + g) * P
+                    nc.tensor.matmul_mx(
+                        bank[:, g, :],
+                        lhsT=en[:, 2 * n0 : 2 * (n0 + P)].bitcast(FP4X4),
+                        lhsT_scale=en_plane[:, n0 : n0 + P],
+                        rhs=codes[:].bitcast(FP8X4),
+                        rhs_scale=plane[:],
+                        start=True,
+                        stop=True,
+                    )
+                nc.scalar.copy(y[:, h0 : h0 + per_bank, :], bank[:])
+            nc.sync.dma_start(out_v[:, :, j0 : j0 + width], y[:])
+
+        vas = [heads(0)]
+        for c in range(CHUNKS):
+            if c + 1 < CHUNKS:
+                vas.append(heads(c + 1))
+            h = ring.tile([P, PACK * CHUNK], BF16, name="h", tag="h", align_bytes=64)
+            for i in range(TILES):
+                part = h[:, PACK * TILE * i : PACK * TILE * (i + 1)]
+                join(c, i, vas[c], part)
+                if c == CHUNKS - 1:
+                    score(part, c * CHUNK + i * TILE, TILE)
+            if c < CHUNKS - 1:
+                score(h[:], c * CHUNK, CHUNK)

@@ -1,6 +1,7 @@
 from contextlib import ExitStack
 
 import concourse.mybir as mybir
+from concourse.masks import make_identity
 
 K, L, R, N, T, J = 1024, 512, 512, 256, 4096, 2048
 FLOPS = 2 * J * R * (K + L + N)
@@ -14,7 +15,8 @@ U8 = mybir.dt.uint8
 FP8X4 = mybir.dt.float8_e4m3fn_x4
 FP4X4 = mybir.dt.float4_e2m1fn_x4
 ABS = mybir.ActivationFunctionType.Abs
-SUB = mybir.AluOpType.subtract
+COPY = mybir.ActivationFunctionType.Copy
+ADD = mybir.AluOpType.add
 
 P = 128
 PACK = 4
@@ -23,6 +25,7 @@ CHUNKS = J // CHUNK
 TILE = 128
 TILES = CHUNK // TILE
 COLS = CHUNK // 16
+TENSOR_TILES = 4
 
 
 def tile_list_kg_absd_none_kernel(
@@ -45,122 +48,139 @@ def tile_list_kg_absd_none_kernel(
         list_a = lists.tile([P, J // 16], U16, name="list_a")
         list_b = lists.tile([P, J // 16], U16, name="list_b")
 
-        tab2_plane = held([P, T], U8, "tab2_plane")
-        wb_plane_raw = held([P, R], U8, "wb_plane_raw")
-        tab_plane = held([P, T], U8, "tab_plane")
-        wa_plane_raw = held([P, 2 * R], U8, "wa_plane_raw")
-        en_plane = held([P, N], U8, "en_plane")
+        shared = ctx.enter_context(tc.tile_pool(name="shared", bufs=1))
+        tab_rows = shared.tile([P, T], U8, name="tab_rows", align_bytes=64, offset=4 * T - 512)
+        wa_plane = held([P, 2 * R], U8, "wa_plane")
         va_planes = [held([P, J], U8, "va_plane%d" % a) for a in range(2)]
-        zero(tab2_plane)
-        nc.vector.memset(tab_plane[32:64, :].bitcast(I32), 0)
-        nc.vector.memset(tab_plane[64:128, :].bitcast(I32), 0)
-        for tile in (wb_plane_raw, wa_plane_raw, en_plane, va_planes[0], va_planes[1]):
-            zero(tile)
+        ident = held([P, P], F32, "ident")
+        nc.vector.memset(tab_rows[64:128, :].bitcast(I32), 0)
+        nc.gpsimd.memset(tab_rows[32:64, :].bitcast(I32), 0)
+        zero(wa_plane)
+        zero(va_planes[0])
+        nc.gpsimd.memset(va_planes[1][:].bitcast(I32), 0)
+        make_identity(nc, ident[:])
 
-        wb_raw = held([P, 2 * R], U8, "wb_raw")
-        tab2_win = held([P, T], U32, "tab2_win")
+        wa = held([P, 4 * R], U8, "wa")
+        tab_win = held([P, T], U32, "tab_win")
         nc.sync.dma_start(list_a[:], offs)
-        nc.sync.dma_start(tab_plane[0:32, :].bitcast(I32), tab_scales.rearrange("a q t -> (a q) t").bitcast(I32))
+        nc.sync.dma_start(tab_rows[0:32, :].bitcast(I32), tab_scales.rearrange("a q t -> (a q) t").bitcast(I32))
         nc.sync.dma_start(list_b[:], offs2)
-        nc.sync.dma_start(wb_raw[:].bitcast(I32), wb_words[0].bitcast(I32))
-        nc.sync.dma_start(tab2_win[:].bitcast(I32), tab2_words[0].rearrange("p t b -> p (t b)").bitcast(I32))
-        for q in range(4):
-            nc.scalar.dma_start(tab2_plane[32 * q : 32 * q + 4, :].bitcast(I32), tab2_scales[0, 4 * q : 4 * q + 4, :].bitcast(I32))
-        for q in range(4):
-            nc.scalar.dma_start(wb_plane_raw[32 * q : 32 * q + 4, :].bitcast(I32), wb_scales[0, 4 * q : 4 * q + 4, :].bitcast(I32))
+        nc.sync.dma_start(tab_win[:].bitcast(I32), tab_words[0].rearrange("p t b -> p (t b)").bitcast(I32))
+        nc.sync.dma_start(wa[:].bitcast(I32).rearrange("p (a c) -> p a c", a=2), wa_words.bitcast(I32).rearrange("a p c -> p a c"))
         for q in range(4):
             nc.sync.dma_start(
-                wa_plane_raw[32 * q : 32 * q + 4, :].bitcast(I32).rearrange("p (a c) -> p a c", a=2),
+                wa_plane[32 * q : 32 * q + 4, :].bitcast(I32).rearrange("p (a c) -> p a c", a=2),
                 wa_scales[:, 4 * q : 4 * q + 4, :].bitcast(I32).rearrange("a p c -> p a c"),
             )
-        for q in range(4):
-            nc.sync.dma_start(en_plane[32 * q : 32 * q + 4, :].bitcast(I32), en_scales[0, 4 * q : 4 * q + 4, :].bitcast(I32))
 
         def gather(window, offsets, c0, c1, dtype, tag):
             got = held([P, (c1 - c0) * CHUNK], dtype, tag)
             nc.vector.tensor_copy(got[:], window[:].indirect(offsets[:, c0 * COLS : c1 * COLS]))
             return got
 
-        def by_slices(raw, passes, dtype, tag):
-            done = held(list(raw.shape), U8, tag)
-            nc.vector.tensor_copy(
-                done[:].bitcast(dtype).rearrange("p (a t m) -> p a t m", a=passes, t=PACK),
-                raw[:].bitcast(dtype).rearrange("p (a m t) -> p a t m", a=passes, t=PACK),
-            )
-            return done
-
-        va_rows = gather(tab_plane, list_a, 0, CHUNKS, U8, "va_rows")
+        va_rows = gather(tab_rows, list_a, 0, CHUNKS, U8, "va_rows")
         for a in range(2):
             for q in range(4):
                 row = 16 * a + 4 * q
                 nc.sync.dma_start(va_planes[a][32 * q : 32 * q + 4, :].bitcast(I32), va_rows[row : row + 4, :].bitcast(I32))
-        vb_planes = [gather(tab2_plane, list_b, c, c + 1, U8, "vb_plane%d" % c) for c in range(2)]
-        wb = by_slices(wb_raw, 1, U16, "wb")
-        wb_plane = by_slices(wb_plane_raw, 1, U8, "wb_plane")
 
-        tab_win = held([P, T], U32, "wb_raw")
-        nc.sync.dma_start(tab_win[:].bitcast(I32), tab_words[0].rearrange("p t b -> p (t b)").bitcast(I32))
-        wa_raw = held([P, 4 * R], U8, "wb_plane_raw")
-        nc.sync.dma_start(wa_raw[:].bitcast(I32).rearrange("p (a c) -> p a c", a=2), wa_words.bitcast(I32).rearrange("a p c -> p a c"))
+        tab2_plane = shared.tile([P, T], U8, name="tab2_plane", align_bytes=64, offset=4 * T + 3 * R + 3 * N)
+        nc.gpsimd.memset(tab2_plane[:].bitcast(I32), 0)
+        for q in range(4):
+            nc.sync.dma_start(tab2_plane[32 * q : 32 * q + 4, :].bitcast(I32), tab2_scales[0, 4 * q : 4 * q + 4, :].bitcast(I32))
+        tab2_win = shared.tile([P, T], U32, name="tab2_win", align_bytes=64, offset=0)
+        nc.sync.dma_start(tab2_win[:].bitcast(I32), tab2_words[0].rearrange("p t b -> p (t b)").bitcast(I32))
 
-        hb_tiles = []
-
-        def relation(c):
-            vb = gather(tab2_win, list_b, c, c + 1, U32, "vb%d" % (c % 2))
-            for i in range(TILES):
-                cols = slice(i * TILE, (i + 1) * TILE)
-                bank = psum.tile([P, PACK, TILE], F32, name="hb_bank", tag="hb_bank", bufs=3)
-                for t in range(PACK):
-                    nc.tensor.matmul_mx(
-                        bank[:, t, :],
-                        lhsT=wb[:, 2 * P * t : 2 * P * (t + 1)].bitcast(FP4X4),
-                        lhsT_scale=wb_plane[:, P * t : P * (t + 1)],
-                        rhs=vb[:, cols].bitcast(FP8X4),
-                        rhs_scale=vb_planes[c][:, cols],
-                        start=True,
-                        stop=True,
-                    )
-                hb = ring.tile([P, TILE, PACK], F32, name="hb", tag="hb", bufs=CHUNKS * TILES)
-                nc.scalar.copy(hb[:], bank[:].rearrange("p t j -> p j t"))
-                hb_tiles.append(hb)
-
-        relation(0)
-        relation(1)
-        for c in (2, 3):
-            vb_planes.append(gather(tab2_plane, list_b, c, c + 1, U8, "vb_plane%d" % (c % 2)))
-            relation(c)
-        wa = by_slices(wa_raw, 2, U16, "wa")
-        wa_plane = by_slices(wa_plane_raw, 2, U8, "wa_plane")
-        en = held([P, 2 * N], U8, "wb_plane_raw")
-        nc.sync.dma_start(en[:].bitcast(I32), en_words[0].bitcast(I32))
+        late = shared.tile([P, 3 * R + 3 * N], U8, name="late", align_bytes=64, offset=4 * T)
+        wb_plane, en_plane = late[:, 0:R], late[:, R : R + N]
+        wb, en = late[:, R + N : 3 * R + N], late[:, 3 * R + N : 3 * R + 3 * N]
+        nc.gpsimd.memset(late[:, 0 : R + N].bitcast(I32), 0)
+        nc.sync.dma_start(wb.bitcast(I32), wb_words[0].bitcast(I32))
+        for q in range(4):
+            nc.sync.dma_start(late[32 * q : 32 * q + 4, 0:R].bitcast(I32), wb_scales[0, 4 * q : 4 * q + 4, :].bitcast(I32))
+        nc.sync.dma_start(en.bitcast(I32), en_words[0].bitcast(I32))
+        for q in range(4):
+            nc.sync.dma_start(late[32 * q : 32 * q + 4, R : R + N].bitcast(I32), en_scales[0, 4 * q : 4 * q + 4, :].bitcast(I32))
         out_v = out.rearrange("(h n) j -> n h j", h=2)
 
-        def heads(c):
+        def by_slices(bank):
+            return bank[:].rearrange("j (m t) -> j t m", t=PACK)
+
+        def by_pairs(bank):
+            return bank[:].rearrange("j (m u e) -> j u m e", u=2, e=2)
+
+        minus_ha = []
+        for c in range(CHUNKS):
             pair = gather(tab_win, list_a, c, c + 1, U32, "va_pair")
-            va = ring.tile([P, 4 * CHUNK], U8, name="va", tag="va", align_bytes=64)
+            va = held([P, 4 * CHUNK], U8, "va%d" % c)
             nc.vector.tensor_copy(
                 va[:].bitcast(U16).rearrange("p (d j) -> p d j", d=2),
                 pair[:].bitcast(U16).rearrange("p (j d) -> p d j", d=2),
             )
-            return va
-
-        def join(c, i, va, h):
-            j0 = c * CHUNK + i * TILE
-            bank = psum.tile([P, PACK, TILE], F32, name="ha_bank", tag="ha_bank", bufs=3)
-            for t in range(PACK):
+            for i in range(TILES):
+                j0 = c * CHUNK + i * TILE
+                bank = psum.tile([P, R], F32, name="sum_bank", tag="sum_bank", bufs=4)
                 for a in range(2):
                     nc.tensor.matmul_mx(
-                        bank[:, t, :],
-                        lhsT=wa[:, 2 * (R * a + P * t) : 2 * (R * a + P * (t + 1))].bitcast(FP4X4),
-                        lhsT_scale=wa_plane[:, R * a + P * t : R * a + P * (t + 1)],
-                        rhs=va[:, 2 * (CHUNK * a + TILE * i) : 2 * (CHUNK * a + TILE * (i + 1))].bitcast(FP4X4),
-                        rhs_scale=va_planes[a][:, j0 : j0 + TILE],
+                        bank[:],
+                        lhsT=va[:, 2 * (CHUNK * a + TILE * i) : 2 * (CHUNK * a + TILE * (i + 1))].bitcast(FP4X4),
+                        lhsT_scale=va_planes[a][:, j0 : j0 + TILE],
+                        rhs=wa[:, 2 * R * a : 2 * R * (a + 1)].bitcast(FP4X4),
+                        rhs_scale=wa_plane[:, R * a : R * (a + 1)],
                         start=(a == 0),
                         stop=(a == 1),
                     )
-            diff = ring.tile([P, TILE, PACK], F32, name="diff", tag="diff", bufs=4)
-            nc.vector.tensor_tensor(diff[:], bank[:].rearrange("p t j -> p j t"), hb_tiles[c * TILES + i][:], SUB)
-            nc.scalar.activation(h, diff[:].rearrange("p j t -> p (j t)"), ABS)
+                neg = ring.tile([P, R], F32, name="neg", tag="neg", bufs=CHUNKS * TILES)
+                if c * TILES + i < TENSOR_TILES:
+                    nc.scalar.activation(neg[:].rearrange("j (t m) -> j t m", t=PACK), by_slices(bank), COPY, scale=-1.0)
+                else:
+                    nc.scalar.activation(neg[:].rearrange("j (u m e) -> j u m e", u=2, e=2), by_pairs(bank), COPY, scale=-1.0)
+                minus_ha.append(neg)
+
+        def relation(n, vb, vb_plane):
+            cols = slice(n % TILES * TILE, (n % TILES + 1) * TILE)
+            bank = psum.tile([P, R], F32, name="sum_bank", tag="sum_bank", bufs=4)
+            nc.tensor.matmul_mx(
+                bank[:],
+                lhsT=vb[:, cols].bitcast(FP8X4),
+                lhsT_scale=vb_plane[:, cols],
+                rhs=wb.bitcast(FP4X4),
+                rhs_scale=wb_plane,
+                start=True,
+                stop=True,
+            )
+            return bank
+
+        def join_on_tensor(n, vb, vb_plane, h):
+            bank = relation(n, vb, vb_plane)
+            hb = ring.tile([P, PACK, P], F32, name="hb", tag="hb")
+            nc.scalar.copy(hb[:], by_slices(bank))
+            turned = psum.tile([P, PACK, TILE], F32, name="turned", tag="turned")
+            for t in range(PACK):
+                nc.tensor.matmul(turned[:, t, :], lhsT=minus_ha[n][:, P * t : P * (t + 1)], rhs=ident[:], is_transpose=True, start=True, stop=False)
+                nc.tensor.matmul(turned[:, t, :], lhsT=hb[:, t, :], rhs=ident[:], is_transpose=True, start=False, stop=True)
+            nc.scalar.activation(h.rearrange("p (j t) -> p j t", t=PACK), turned[:].rearrange("p t j -> p j t"), ABS)
+
+        def join_on_vector(n0, count, vb, vb_plane, h):
+            diff = ring.tile([P, count, R], BF16, name="diff", tag="diff", bufs=3)
+            for g in range(count):
+                bank = relation(n0 + g, vb, vb_plane)
+                nc.vector.tensor_tensor(
+                    diff[:, g, :].rearrange("j (u m e) -> j u m e", u=2, e=2),
+                    by_pairs(bank),
+                    minus_ha[n0 + g][:].rearrange("j (u m e) -> j u m e", u=2, e=2),
+                    ADD,
+                )
+            turned = psum.tile([P, 2, count * TILE], F32, name="turned", tag="turned")
+            words = diff[:].bitcast(F32)
+            for g in range(count):
+                for u in range(2):
+                    nc.tensor.transpose(turned[:, u, g * TILE : (g + 1) * TILE], words[:, g, P * u : P * (u + 1)], ident[:])
+            nc.scalar.activation(
+                h.rearrange("p (j u e) -> p j u e", u=2, e=2),
+                turned[:].bitcast(BF16).rearrange("p u (j e) -> p j u e", e=2),
+                ABS,
+            )
 
         def score(h, j0, width):
             codes = ring.tile([P, width], U32, name="codes", tag="codes", align_bytes=64, bufs=3)
@@ -184,15 +204,20 @@ def tile_list_kg_absd_none_kernel(
                 nc.scalar.copy(y[:, h0 : h0 + per_bank, :], bank[:])
             nc.sync.dma_start(out_v[:, :, j0 : j0 + width], y[:])
 
-        vas = [heads(0)]
         for c in range(CHUNKS):
-            if c + 1 < CHUNKS:
-                vas.append(heads(c + 1))
+            vb_plane = gather(tab2_plane, list_b, c, c + 1, U8, "vb_plane%d" % (c % 2))
+            vb = gather(tab2_win, list_b, c, c + 1, U32, "vb%d" % (c % 2))
             h = ring.tile([P, PACK * CHUNK], BF16, name="h", tag="h", align_bytes=64)
-            for i in range(TILES):
-                part = h[:, PACK * TILE * i : PACK * TILE * (i + 1)]
-                join(c, i, vas[c], part)
-                if c == CHUNKS - 1:
-                    score(part, c * CHUNK + i * TILE, TILE)
-            if c < CHUNKS - 1:
+            last = c == CHUNKS - 1
+            i = 0
+            for count in (1, 1, 1, 1) if c * TILES < TENSOR_TILES else (2, 1, 1) if last else (2, 2):
+                part = h[:, PACK * TILE * i : PACK * TILE * (i + count)]
+                if c * TILES < TENSOR_TILES:
+                    join_on_tensor(c * TILES + i, vb, vb_plane, part)
+                else:
+                    join_on_vector(c * TILES + i, count, vb, vb_plane, part)
+                if last:
+                    score(part, c * CHUNK + i * TILE, count * TILE)
+                i = i + count
+            if not last:
                 score(h[:], c * CHUNK, CHUNK)

@@ -16,7 +16,7 @@ FP8X4 = mybir.dt.float8_e4m3fn_x4
 FP4X4 = mybir.dt.float4_e2m1fn_x4
 ABS = mybir.ActivationFunctionType.Abs
 COPY = mybir.ActivationFunctionType.Copy
-ADD = mybir.AluOpType.add
+SUB = mybir.AluOpType.subtract
 
 P = 128
 PACK = 4
@@ -25,7 +25,13 @@ CHUNKS = J // CHUNK
 TILE = 128
 TILES = CHUNK // TILE
 COLS = CHUNK // 16
-TENSOR_TILES = 4
+TENSOR_TILES = (4,8)
+BANKS = 4 * (("sum_bank", 4),) + 2 * (("turned", 2),) + 2 * (("y_bank", 2),)
+LAG = 3
+SLOTS = 5
+SLOT_BYTES = 2048
+VECTOR_EMPTIES = (8,9)
+GROUPS = (2,2,1,2,1,1,2,1,2,1,1)
 
 
 def tile_list_kg_absd_none_kernel(
@@ -49,128 +55,130 @@ def tile_list_kg_absd_none_kernel(
         list_b = lists.tile([P, J // 16], U16, name="list_b")
 
         shared = ctx.enter_context(tc.tile_pool(name="shared", bufs=1))
-        tab_rows = shared.tile([P, T], U8, name="tab_rows", align_bytes=64, offset=4 * T - 512)
+        tab_rows = shared.tile([P, T], U8, name="tab_rows", align_bytes=64, offset=4 * T - 1024)
+        tab2_plane = held([P, T], U8, "tab2_plane")
+        wb_plane = held([P, R], U8, "wb_plane")
         wa_plane = held([P, 2 * R], U8, "wa_plane")
-        va_planes = [held([P, J], U8, "va_plane%d" % a) for a in range(2)]
+        en_plane = held([P, N], U8, "en_plane")
+        va_planes = held([P, 2 * J], U8, "va_planes")
         ident = held([P, P], F32, "ident")
-        nc.vector.memset(tab_rows[64:128, :].bitcast(I32), 0)
-        nc.gpsimd.memset(tab_rows[32:64, :].bitcast(I32), 0)
-        zero(wa_plane)
-        zero(va_planes[0])
-        nc.gpsimd.memset(va_planes[1][:].bitcast(I32), 0)
-        make_identity(nc, ident[:])
+        zero(tab2_plane)
+        nc.vector.memset(tab_rows[0:96, :].bitcast(I32), 0)
 
-        wa = held([P, 4 * R], U8, "wa")
-        tab_win = held([P, T], U32, "tab_win")
+        tab2_win = held([P, T], U32, "tab2_win")
+        wb = held([P, 2 * R], U8, "wb")
         nc.sync.dma_start(list_a[:], offs)
-        nc.sync.dma_start(tab_rows[0:32, :].bitcast(I32), tab_scales.rearrange("a q t -> (a q) t").bitcast(I32))
+        nc.sync.dma_start(tab_rows[96:128, :].bitcast(I32), tab_scales.rearrange("a q t -> (a q) t").bitcast(I32))
         nc.sync.dma_start(list_b[:], offs2)
-        nc.sync.dma_start(tab_win[:].bitcast(I32), tab_words[0].rearrange("p t b -> p (t b)").bitcast(I32))
-        nc.sync.dma_start(wa[:].bitcast(I32).rearrange("p (a c) -> p a c", a=2), wa_words.bitcast(I32).rearrange("a p c -> p a c"))
+        nc.sync.dma_start(wb[:].bitcast(I32), wb_words[0].bitcast(I32))
+        nc.sync.dma_start(tab2_win[:].bitcast(I32), tab2_words[0].rearrange("p t b -> p (t b)").bitcast(I32))
         for q in range(4):
-            nc.sync.dma_start(
+            nc.scalar.dma_start(tab2_plane[32 * q : 32 * q + 4, :].bitcast(I32), tab2_scales[0, 4 * q : 4 * q + 4, :].bitcast(I32))
+
+        for plane in (wb_plane, wa_plane, en_plane):
+            nc.gpsimd.memset(plane[:].bitcast(I32), 0)
+        for q in range(4):
+            nc.gpsimd.dma_start(wb_plane[32 * q : 32 * q + 4, :].bitcast(I32), wb_scales[0, 4 * q : 4 * q + 4, :].bitcast(I32))
+        nc.gpsimd.memset(va_planes[:].bitcast(I32), 0)
+        for q in range(4):
+            nc.gpsimd.dma_start(
                 wa_plane[32 * q : 32 * q + 4, :].bitcast(I32).rearrange("p (a c) -> p a c", a=2),
                 wa_scales[:, 4 * q : 4 * q + 4, :].bitcast(I32).rearrange("a p c -> p a c"),
             )
+        make_identity(nc, ident[:])
+        for q in range(4):
+            nc.gpsimd.dma_start(en_plane[32 * q : 32 * q + 4, :].bitcast(I32), en_scales[0, 4 * q : 4 * q + 4, :].bitcast(I32))
 
-        def gather(window, offsets, c0, c1, dtype, tag):
-            got = held([P, (c1 - c0) * CHUNK], dtype, tag)
+        def gather(got, window, offsets, c0, c1):
             nc.vector.tensor_copy(got[:], window[:].indirect(offsets[:, c0 * COLS : c1 * COLS]))
-            return got
 
-        va_rows = gather(tab_rows, list_a, 0, CHUNKS, U8, "va_rows")
+        va_rows = held([P, J], U8, "va_rows")
+        gather(va_rows, tab_rows, list_a, 0, CHUNKS)
+
+        tab_win = shared.tile([P, T], U32, name="tab_win", align_bytes=64, offset=0)
+        en = shared.tile([P, 2 * N], U8, name="en", align_bytes=64, offset=4 * T)
+        wa = shared.tile([P, 4 * R], U8, name="wa", align_bytes=64, offset=4 * T + 2 * N)
+        nc.sync.dma_start(tab_win[:].bitcast(I32), tab_words[0].rearrange("p t b -> p (t b)").bitcast(I32))
+        nc.sync.dma_start(wa[:].bitcast(I32).rearrange("p (a c) -> p a c", a=2), wa_words.bitcast(I32).rearrange("a p c -> p a c"))
         for a in range(2):
             for q in range(4):
-                row = 16 * a + 4 * q
-                nc.sync.dma_start(va_planes[a][32 * q : 32 * q + 4, :].bitcast(I32), va_rows[row : row + 4, :].bitcast(I32))
-
-        tab2_plane = shared.tile([P, T], U8, name="tab2_plane", align_bytes=64, offset=4 * T + 3 * R + 3 * N)
-        nc.gpsimd.memset(tab2_plane[:].bitcast(I32), 0)
-        for q in range(4):
-            nc.sync.dma_start(tab2_plane[32 * q : 32 * q + 4, :].bitcast(I32), tab2_scales[0, 4 * q : 4 * q + 4, :].bitcast(I32))
-        tab2_win = shared.tile([P, T], U32, name="tab2_win", align_bytes=64, offset=0)
-        nc.sync.dma_start(tab2_win[:].bitcast(I32), tab2_words[0].rearrange("p t b -> p (t b)").bitcast(I32))
-
-        late = shared.tile([P, 3 * R + 3 * N], U8, name="late", align_bytes=64, offset=4 * T)
-        wb_plane, en_plane = late[:, 0:R], late[:, R : R + N]
-        wb, en = late[:, R + N : 3 * R + N], late[:, 3 * R + N : 3 * R + 3 * N]
-        nc.gpsimd.memset(late[:, 0 : R + N].bitcast(I32), 0)
-        nc.sync.dma_start(wb.bitcast(I32), wb_words[0].bitcast(I32))
-        for q in range(4):
-            nc.sync.dma_start(late[32 * q : 32 * q + 4, 0:R].bitcast(I32), wb_scales[0, 4 * q : 4 * q + 4, :].bitcast(I32))
-        nc.sync.dma_start(en.bitcast(I32), en_words[0].bitcast(I32))
-        for q in range(4):
-            nc.sync.dma_start(late[32 * q : 32 * q + 4, R : R + N].bitcast(I32), en_scales[0, 4 * q : 4 * q + 4, :].bitcast(I32))
+                row = 96 + 16 * a + 4 * q
+                nc.sync.dma_start(
+                    va_planes[32 * q : 32 * q + 4, J * a : J * (a + 1)].bitcast(I32), va_rows[row : row + 4, :].bitcast(I32)
+                )
+        nc.sync.dma_start(en[:].bitcast(I32), en_words[0].bitcast(I32))
         out_v = out.rearrange("(h n) j -> n h j", h=2)
-
-        def by_slices(bank):
-            return bank[:].rearrange("j (m t) -> j t m", t=PACK)
 
         def by_pairs(bank):
             return bank[:].rearrange("j (m u e) -> j u m e", u=2, e=2)
 
-        minus_ha = []
+        def as_pairs(ap):
+            return ap.rearrange("j (u m e) -> j u m e", u=2, e=2)
+
+        def by_slices(bank):
+            return bank[:].rearrange("j (m t) -> j t m", t=PACK)
+
+        def as_slices(ap):
+            return ap.rearrange("j (t m) -> j t m", t=PACK)
+
+        hb_tiles = []
         for c in range(CHUNKS):
-            pair = gather(tab_win, list_a, c, c + 1, U32, "va_pair")
-            va = held([P, 4 * CHUNK], U8, "va%d" % c)
+            vb_plane = ring.tile([P, CHUNK], U8, name="vb_plane", tag="vb_plane", align_bytes=64)
+            gather(vb_plane, tab2_plane, list_b, c, c + 1)
+            vb = held([P, CHUNK], U32, "vb%d" % c)
+            gather(vb, tab2_win, list_b, c, c + 1)
+            for i in range(TILES):
+                cols = slice(i * TILE, (i + 1) * TILE)
+                tag, bufs = BANKS[(c * TILES + i) % len(BANKS)]
+                bank = psum.tile([P, R], F32, name=tag, tag=tag, bufs=bufs)
+                nc.tensor.matmul_mx(
+                    bank[:],
+                    lhsT=vb[:, cols].bitcast(FP8X4),
+                    lhsT_scale=vb_plane[:, cols],
+                    rhs=wb[:].bitcast(FP4X4),
+                    rhs_scale=wb_plane[:],
+                    start=True,
+                    stop=True,
+                )
+                hb = ring.tile([P, R], F32, name="hb", tag="hb", bufs=CHUNKS * TILES)
+                if c * TILES + i in TENSOR_TILES:
+                    nc.scalar.activation(as_slices(hb[:]), by_slices(bank), COPY, scale=-1.0)
+                else:
+                    nc.scalar.copy(as_pairs(hb[:]), by_pairs(bank))
+                hb_tiles.append(hb)
+
+        def look_up(c):
+            pair = held([P, CHUNK], U32, "va_pair")
+            gather(pair, tab_win, list_a, c, c + 1)
+            return pair
+
+        def part_words(pair):
+            va = held([P, 4 * CHUNK], U8, "va")
             nc.vector.tensor_copy(
                 va[:].bitcast(U16).rearrange("p (d j) -> p d j", d=2),
                 pair[:].bitcast(U16).rearrange("p (j d) -> p d j", d=2),
             )
-            for i in range(TILES):
-                j0 = c * CHUNK + i * TILE
-                bank = psum.tile([P, R], F32, name="sum_bank", tag="sum_bank", bufs=4)
-                for a in range(2):
-                    nc.tensor.matmul_mx(
-                        bank[:],
-                        lhsT=va[:, 2 * (CHUNK * a + TILE * i) : 2 * (CHUNK * a + TILE * (i + 1))].bitcast(FP4X4),
-                        lhsT_scale=va_planes[a][:, j0 : j0 + TILE],
-                        rhs=wa[:, 2 * R * a : 2 * R * (a + 1)].bitcast(FP4X4),
-                        rhs_scale=wa_plane[:, R * a : R * (a + 1)],
-                        start=(a == 0),
-                        stop=(a == 1),
-                    )
-                neg = ring.tile([P, R], F32, name="neg", tag="neg", bufs=CHUNKS * TILES)
-                if c * TILES + i < TENSOR_TILES:
-                    nc.scalar.activation(neg[:].rearrange("j (t m) -> j t m", t=PACK), by_slices(bank), COPY, scale=-1.0)
-                else:
-                    nc.scalar.activation(neg[:].rearrange("j (u m e) -> j u m e", u=2, e=2), by_pairs(bank), COPY, scale=-1.0)
-                minus_ha.append(neg)
+            return va
 
-        def relation(n, vb, vb_plane):
-            cols = slice(n % TILES * TILE, (n % TILES + 1) * TILE)
+        def head(n, va):
+            i = n % TILES
             bank = psum.tile([P, R], F32, name="sum_bank", tag="sum_bank", bufs=4)
-            nc.tensor.matmul_mx(
-                bank[:],
-                lhsT=vb[:, cols].bitcast(FP8X4),
-                lhsT_scale=vb_plane[:, cols],
-                rhs=wb.bitcast(FP4X4),
-                rhs_scale=wb_plane,
-                start=True,
-                stop=True,
-            )
+            for a in range(2):
+                nc.tensor.matmul_mx(
+                    bank[:],
+                    lhsT=va[:, 2 * (CHUNK * a + TILE * i) : 2 * (CHUNK * a + TILE * (i + 1))].bitcast(FP4X4),
+                    lhsT_scale=va_planes[:, J * a + n * TILE : J * a + (n + 1) * TILE],
+                    rhs=wa[:, 2 * R * a : 2 * R * (a + 1)].bitcast(FP4X4),
+                    rhs_scale=wa_plane[:, R * a : R * (a + 1)],
+                    start=(a == 0),
+                    stop=(a == 1),
+                )
             return bank
 
-        def join_on_tensor(n, vb, vb_plane, h):
-            bank = relation(n, vb, vb_plane)
-            hb = ring.tile([P, PACK, P], F32, name="hb", tag="hb")
-            nc.scalar.copy(hb[:], by_slices(bank))
-            turned = psum.tile([P, PACK, TILE], F32, name="turned", tag="turned")
-            for t in range(PACK):
-                nc.tensor.matmul(turned[:, t, :], lhsT=minus_ha[n][:, P * t : P * (t + 1)], rhs=ident[:], is_transpose=True, start=True, stop=False)
-                nc.tensor.matmul(turned[:, t, :], lhsT=hb[:, t, :], rhs=ident[:], is_transpose=True, start=False, stop=True)
-            nc.scalar.activation(h.rearrange("p (j t) -> p j t", t=PACK), turned[:].rearrange("p t j -> p j t"), ABS)
+        def subtract(diff, bank, hb):
+            nc.vector.tensor_tensor(as_pairs(diff), by_pairs(bank), as_pairs(hb[:]), SUB)
 
-        def join_on_vector(n0, count, vb, vb_plane, h):
-            diff = ring.tile([P, count, R], BF16, name="diff", tag="diff", bufs=3)
-            for g in range(count):
-                bank = relation(n0 + g, vb, vb_plane)
-                nc.vector.tensor_tensor(
-                    diff[:, g, :].rearrange("j (u m e) -> j u m e", u=2, e=2),
-                    by_pairs(bank),
-                    minus_ha[n0 + g][:].rearrange("j (u m e) -> j u m e", u=2, e=2),
-                    ADD,
-                )
+        def turn(diff, count, h):
             turned = psum.tile([P, 2, count * TILE], F32, name="turned", tag="turned")
             words = diff[:].bitcast(F32)
             for g in range(count):
@@ -182,7 +190,17 @@ def tile_list_kg_absd_none_kernel(
                 ABS,
             )
 
-        def score(h, j0, width):
+        def turn_and_add(bank, minus_hb, h):
+            ha = ring.tile([P, R], F32, name="ha", tag="ha")
+            nc.scalar.copy(as_slices(ha[:]), by_slices(bank))
+            turned = psum.tile([P, PACK, TILE], F32, name="turned", tag="turned")
+            for t in range(PACK):
+                cols = slice(P * t, P * (t + 1))
+                nc.tensor.matmul(turned[:, t, :], lhsT=minus_hb[:, cols], rhs=ident[:], is_transpose=True, start=True, stop=False)
+                nc.tensor.matmul(turned[:, t, :], lhsT=ha[:, cols], rhs=ident[:], is_transpose=True, start=False, stop=True)
+            nc.scalar.activation(h.rearrange("p (j t) -> p j t", t=PACK), turned[:].rearrange("p t j -> p j t"), ABS)
+
+        def score(h, j0, width, empty):
             codes = ring.tile([P, width], U32, name="codes", tag="codes", align_bytes=64, bufs=3)
             plane = ring.tile([P, width], U8, name="plane", tag="plane", align_bytes=64, bufs=3)
             nc.vector.quantize_mx(codes[:].bitcast(FP8X4), plane[:], h)
@@ -201,23 +219,39 @@ def tile_list_kg_absd_none_kernel(
                         start=True,
                         stop=True,
                     )
-                nc.scalar.copy(y[:, h0 : h0 + per_bank, :], bank[:])
+                empty(y[:, h0 : h0 + per_bank, :], bank[:])
             nc.sync.dma_start(out_v[:, :, j0 : j0 + width], y[:])
 
-        for c in range(CHUNKS):
-            vb_plane = gather(tab2_plane, list_b, c, c + 1, U8, "vb_plane%d" % (c % 2))
-            vb = gather(tab2_win, list_b, c, c + 1, U32, "vb%d" % (c % 2))
-            h = ring.tile([P, PACK * CHUNK], BF16, name="h", tag="h", align_bytes=64)
-            last = c == CHUNKS - 1
-            i = 0
-            for count in (1, 1, 1, 1) if c * TILES < TENSOR_TILES else (2, 1, 1) if last else (2, 2):
-                part = h[:, PACK * TILE * i : PACK * TILE * (i + count)]
-                if c * TILES < TENSOR_TILES:
-                    join_on_tensor(c * TILES + i, vb, vb_plane, part)
-                else:
-                    join_on_vector(c * TILES + i, count, vb, vb_plane, part)
-                if last:
-                    score(part, c * CHUNK + i * TILE, count * TILE)
-                i = i + count
-            if not last:
-                score(h[:], c * CHUNK, CHUNK)
+        turns = ctx.enter_context(tc.tile_pool(name="turns", bufs=1))
+
+        def slot(shape, name, g):
+            return turns.tile(shape, BF16, name="%s%d" % (name, g), align_bytes=64, offset=SLOT_BYTES * (g % SLOTS))
+
+        va = part_words(look_up(0))
+        pair = look_up(1)
+        banks = [head(n, va) for n in range(TILES)]
+        parted = 1
+        waiting = []
+        n0 = 0
+        for g, count in enumerate(GROUPS):
+            while len(waiting) > LAG - 1:
+                score(*waiting.pop(0))
+            h = slot([P, PACK * TILE * count], "h", g + LAG)
+            if n0 in TENSOR_TILES:
+                turn_and_add(banks[n0], hb_tiles[n0], h[:])
+            else:
+                diff = slot([P, count, R], "diff", g)
+                for i in range(count):
+                    subtract(diff[:, i, :], banks[n0 + i], hb_tiles[n0 + i])
+                if parted == n0 // TILES + 1 and parted < CHUNKS:
+                    va = part_words(pair)
+                    parted = parted + 1
+                    if parted < CHUNKS:
+                        pair = look_up(parted)
+                turn(diff, count, h[:])
+                banks.extend([head(n, va) for n in range(len(banks), min(n0 + count + TILES, parted * TILES))])
+            empty = nc.vector.tensor_copy if g in VECTOR_EMPTIES else nc.scalar.copy
+            waiting.append((h[:], n0 * TILE, count * TILE, empty))
+            n0 = n0 + count
+        for left in waiting:
+            score(*left)

@@ -25,13 +25,13 @@ CHUNKS = J // CHUNK
 TILE = 128
 TILES = CHUNK // TILE
 COLS = CHUNK // 16
-TENSOR_TILES = (4,8)
+TENSOR_TILES = (0, 4, 8)
 BANKS = 4 * (("sum_bank", 4),) + 2 * (("turned", 2),) + 2 * (("y_bank", 2),)
 LAG = 3
 SLOTS = 5
 SLOT_BYTES = 2048
-VECTOR_EMPTIES = (8,9)
-GROUPS = (2,2,1,2,1,1,2,1,2,1,1)
+VECTOR_EMPTIES = (8, 9)
+GROUPS = (1, 2, 1, 1, 2, 1, 1, 2, 1, 2, 1, 1)
 
 
 def tile_list_kg_absd_none_kernel(

from contextlib import ExitStack

import concourse.mybir as mybir
from concourse.masks import make_identity

K, L, R, N, T, J = 1024, 512, 512, 256, 4096, 2048
FLOPS = 2 * J * R * (K + L + N)

F32 = mybir.dt.float32
BF16 = mybir.dt.bfloat16
I32 = mybir.dt.int32
U32 = mybir.dt.uint32
U16 = mybir.dt.uint16
U8 = mybir.dt.uint8
FP8X4 = mybir.dt.float8_e4m3fn_x4
FP4X4 = mybir.dt.float4_e2m1fn_x4
ABS = mybir.ActivationFunctionType.Abs
COPY = mybir.ActivationFunctionType.Copy
SUB = mybir.AluOpType.subtract

P = 128
PACK = 4
CHUNK = 512
CHUNKS = J // CHUNK
TILE = 128
TILES = CHUNK // TILE
COLS = CHUNK // 16
TENSOR_TILES = (0, 4, 8)
BANKS = 4 * (("sum_bank", 4),) + 2 * (("turned", 2),) + 2 * (("y_bank", 2),)
LAG = 3
SLOTS = 5
SLOT_BYTES = 2048
VECTOR_EMPTIES = (8, 9)
GROUPS = (1, 2, 1, 1, 2, 1, 1, 2, 1, 2, 1, 1)


def tile_list_kg_absd_none_kernel(
    tc, tab_words, tab_scales, tab2_words, tab2_scales, wa_words, wa_scales, wb_words, wb_scales,
    en_words, en_scales, offs, offs2, out,
):
    nc = tc.nc
    with ExitStack() as ctx:
        lists = ctx.enter_context(tc.tile_pool(name="lists", bufs=1))
        keep = ctx.enter_context(tc.tile_pool(name="keep", bufs=1))
        ring = ctx.enter_context(tc.tile_pool(name="ring", bufs=2))
        psum = ctx.enter_context(tc.psum_pool(name="psum", bufs=2))

        def held(shape, dtype, tag):
            return keep.tile(shape, dtype, name=tag, tag=tag, align_bytes=64)

        def zero(tile):
            nc.vector.memset(tile[:].bitcast(I32), 0)

        list_a = lists.tile([P, J // 16], U16, name="list_a")
        list_b = lists.tile([P, J // 16], U16, name="list_b")

        shared = ctx.enter_context(tc.tile_pool(name="shared", bufs=1))
        tab_rows = shared.tile([P, T], U8, name="tab_rows", align_bytes=64, offset=4 * T - 1024)
        tab2_plane = held([P, T], U8, "tab2_plane")
        wb_plane = held([P, R], U8, "wb_plane")
        wa_plane = held([P, 2 * R], U8, "wa_plane")
        en_plane = held([P, N], U8, "en_plane")
        va_planes = held([P, 2 * J], U8, "va_planes")
        ident = held([P, P], F32, "ident")
        zero(tab2_plane)
        nc.vector.memset(tab_rows[0:96, :].bitcast(I32), 0)

        tab2_win = held([P, T], U32, "tab2_win")
        wb = held([P, 2 * R], U8, "wb")
        nc.sync.dma_start(list_a[:], offs)
        nc.sync.dma_start(tab_rows[96:128, :].bitcast(I32), tab_scales.rearrange("a q t -> (a q) t").bitcast(I32))
        nc.sync.dma_start(list_b[:], offs2)
        nc.sync.dma_start(wb[:].bitcast(I32), wb_words[0].bitcast(I32))
        nc.sync.dma_start(tab2_win[:].bitcast(I32), tab2_words[0].rearrange("p t b -> p (t b)").bitcast(I32))
        for q in range(4):
            nc.scalar.dma_start(tab2_plane[32 * q : 32 * q + 4, :].bitcast(I32), tab2_scales[0, 4 * q : 4 * q + 4, :].bitcast(I32))

        for plane in (wb_plane, wa_plane, en_plane):
            nc.gpsimd.memset(plane[:].bitcast(I32), 0)
        for q in range(4):
            nc.gpsimd.dma_start(wb_plane[32 * q : 32 * q + 4, :].bitcast(I32), wb_scales[0, 4 * q : 4 * q + 4, :].bitcast(I32))
        nc.gpsimd.memset(va_planes[:].bitcast(I32), 0)
        for q in range(4):
            nc.gpsimd.dma_start(
                wa_plane[32 * q : 32 * q + 4, :].bitcast(I32).rearrange("p (a c) -> p a c", a=2),
                wa_scales[:, 4 * q : 4 * q + 4, :].bitcast(I32).rearrange("a p c -> p a c"),
            )
        make_identity(nc, ident[:])
        for q in range(4):
            nc.gpsimd.dma_start(en_plane[32 * q : 32 * q + 4, :].bitcast(I32), en_scales[0, 4 * q : 4 * q + 4, :].bitcast(I32))

        def gather(got, window, offsets, c0, c1):
            nc.vector.tensor_copy(got[:], window[:].indirect(offsets[:, c0 * COLS : c1 * COLS]))

        va_rows = held([P, J], U8, "va_rows")
        gather(va_rows, tab_rows, list_a, 0, CHUNKS)

        tab_win = shared.tile([P, T], U32, name="tab_win", align_bytes=64, offset=0)
        en = shared.tile([P, 2 * N], U8, name="en", align_bytes=64, offset=4 * T)
        wa = shared.tile([P, 4 * R], U8, name="wa", align_bytes=64, offset=4 * T + 2 * N)
        nc.sync.dma_start(tab_win[:].bitcast(I32), tab_words[0].rearrange("p t b -> p (t b)").bitcast(I32))
        nc.sync.dma_start(wa[:].bitcast(I32).rearrange("p (a c) -> p a c", a=2), wa_words.bitcast(I32).rearrange("a p c -> p a c"))
        for a in range(2):
            for q in range(4):
                row = 96 + 16 * a + 4 * q
                nc.sync.dma_start(
                    va_planes[32 * q : 32 * q + 4, J * a : J * (a + 1)].bitcast(I32), va_rows[row : row + 4, :].bitcast(I32)
                )
        nc.sync.dma_start(en[:].bitcast(I32), en_words[0].bitcast(I32))
        out_v = out.rearrange("(h n) j -> n h j", h=2)

        def by_pairs(bank):
            return bank[:].rearrange("j (m u e) -> j u m e", u=2, e=2)

        def as_pairs(ap):
            return ap.rearrange("j (u m e) -> j u m e", u=2, e=2)

        def by_slices(bank):
            return bank[:].rearrange("j (m t) -> j t m", t=PACK)

        def as_slices(ap):
            return ap.rearrange("j (t m) -> j t m", t=PACK)

        hb_tiles = []
        for c in range(CHUNKS):
            vb_plane = ring.tile([P, CHUNK], U8, name="vb_plane", tag="vb_plane", align_bytes=64)
            gather(vb_plane, tab2_plane, list_b, c, c + 1)
            vb = held([P, CHUNK], U32, "vb%d" % c)
            gather(vb, tab2_win, list_b, c, c + 1)
            for i in range(TILES):
                cols = slice(i * TILE, (i + 1) * TILE)
                tag, bufs = BANKS[(c * TILES + i) % len(BANKS)]
                bank = psum.tile([P, R], F32, name=tag, tag=tag, bufs=bufs)
                nc.tensor.matmul_mx(
                    bank[:],
                    lhsT=vb[:, cols].bitcast(FP8X4),
                    lhsT_scale=vb_plane[:, cols],
                    rhs=wb[:].bitcast(FP4X4),
                    rhs_scale=wb_plane[:],
                    start=True,
                    stop=True,
                )
                hb = ring.tile([P, R], F32, name="hb", tag="hb", bufs=CHUNKS * TILES)
                if c * TILES + i in TENSOR_TILES:
                    nc.scalar.activation(as_slices(hb[:]), by_slices(bank), COPY, scale=-1.0)
                else:
                    nc.scalar.copy(as_pairs(hb[:]), by_pairs(bank))
                hb_tiles.append(hb)

        def look_up(c):
            pair = held([P, CHUNK], U32, "va_pair")
            gather(pair, tab_win, list_a, c, c + 1)
            return pair

        def part_words(pair):
            va = held([P, 4 * CHUNK], U8, "va")
            nc.vector.tensor_copy(
                va[:].bitcast(U16).rearrange("p (d j) -> p d j", d=2),
                pair[:].bitcast(U16).rearrange("p (j d) -> p d j", d=2),
            )
            return va

        def head(n, va):
            i = n % TILES
            bank = psum.tile([P, R], F32, name="sum_bank", tag="sum_bank", bufs=4)
            for a in range(2):
                nc.tensor.matmul_mx(
                    bank[:],
                    lhsT=va[:, 2 * (CHUNK * a + TILE * i) : 2 * (CHUNK * a + TILE * (i + 1))].bitcast(FP4X4),
                    lhsT_scale=va_planes[:, J * a + n * TILE : J * a + (n + 1) * TILE],
                    rhs=wa[:, 2 * R * a : 2 * R * (a + 1)].bitcast(FP4X4),
                    rhs_scale=wa_plane[:, R * a : R * (a + 1)],
                    start=(a == 0),
                    stop=(a == 1),
                )
            return bank

        def subtract(diff, bank, hb):
            nc.vector.tensor_tensor(as_pairs(diff), by_pairs(bank), as_pairs(hb[:]), SUB)

        def turn(diff, count, h):
            turned = psum.tile([P, 2, count * TILE], F32, name="turned", tag="turned")
            words = diff[:].bitcast(F32)
            for g in range(count):
                for u in range(2):
                    nc.tensor.transpose(turned[:, u, g * TILE : (g + 1) * TILE], words[:, g, P * u : P * (u + 1)], ident[:])
            nc.scalar.activation(
                h.rearrange("p (j u e) -> p j u e", u=2, e=2),
                turned[:].bitcast(BF16).rearrange("p u (j e) -> p j u e", e=2),
                ABS,
            )

        def turn_and_add(bank, minus_hb, h):
            ha = ring.tile([P, R], F32, name="ha", tag="ha")
            nc.scalar.copy(as_slices(ha[:]), by_slices(bank))
            turned = psum.tile([P, PACK, TILE], F32, name="turned", tag="turned")
            for t in range(PACK):
                cols = slice(P * t, P * (t + 1))
                nc.tensor.matmul(turned[:, t, :], lhsT=minus_hb[:, cols], rhs=ident[:], is_transpose=True, start=True, stop=False)
                nc.tensor.matmul(turned[:, t, :], lhsT=ha[:, cols], rhs=ident[:], is_transpose=True, start=False, stop=True)
            nc.scalar.activation(h.rearrange("p (j t) -> p j t", t=PACK), turned[:].rearrange("p t j -> p j t"), ABS)

        def score(h, j0, width, empty):
            codes = ring.tile([P, width], U32, name="codes", tag="codes", align_bytes=64, bufs=3)
            plane = ring.tile([P, width], U8, name="plane", tag="plane", align_bytes=64, bufs=3)
            nc.vector.quantize_mx(codes[:].bitcast(FP8X4), plane[:], h)
            y = ring.tile([P, 2, width], F32, name="y", tag="y", bufs=3)
            per_bank = min(2, 512 // width)
            for h0 in range(0, 2, per_bank):
                bank = psum.tile([P, per_bank, width], F32, name="y_bank", tag="y_bank")
                for g in range(per_bank):
                    n0 = (h0 + g) * P
                    nc.tensor.matmul_mx(
                        bank[:, g, :],
                        lhsT=en[:, 2 * n0 : 2 * (n0 + P)].bitcast(FP4X4),
                        lhsT_scale=en_plane[:, n0 : n0 + P],
                        rhs=codes[:].bitcast(FP8X4),
                        rhs_scale=plane[:],
                        start=True,
                        stop=True,
                    )
                empty(y[:, h0 : h0 + per_bank, :], bank[:])
            nc.sync.dma_start(out_v[:, :, j0 : j0 + width], y[:])

        turns = ctx.enter_context(tc.tile_pool(name="turns", bufs=1))

        def slot(shape, name, g):
            return turns.tile(shape, BF16, name="%s%d" % (name, g), align_bytes=64, offset=SLOT_BYTES * (g % SLOTS))

        va = part_words(look_up(0))
        pair = look_up(1)
        banks = [head(n, va) for n in range(TILES)]
        parted = 1
        waiting = []
        n0 = 0
        for g, count in enumerate(GROUPS):
            while len(waiting) > LAG - 1:
                score(*waiting.pop(0))
            h = slot([P, PACK * TILE * count], "h", g + LAG)
            if n0 in TENSOR_TILES:
                turn_and_add(banks[n0], hb_tiles[n0], h[:])
            else:
                diff = slot([P, count, R], "diff", g)
                for i in range(count):
                    subtract(diff[:, i, :], banks[n0 + i], hb_tiles[n0 + i])
                if parted == n0 // TILES + 1 and parted < CHUNKS:
                    va = part_words(pair)
                    parted = parted + 1
                    if parted < CHUNKS:
                        pair = look_up(parted)
                turn(diff, count, h[:])
                banks.extend([head(n, va) for n in range(len(banks), min(n0 + count + TILES, parted * TILES))])
            empty = nc.vector.tensor_copy if g in VECTOR_EMPTIES else nc.scalar.copy
            waiting.append((h[:], n0 * TILE, count * TILE, empty))
            n0 = n0 + count
        for left in waiting:
            score(*left)
